import numpy as np
import ml_dtypes


def mxq(x, axis, fmt="e4m3"):
    dtype, down = {"e4m3": (ml_dtypes.float8_e4m3fn, 7), "e5m2": (ml_dtypes.float8_e5m2, 14)}[fmt]
    v = np.moveaxis(np.asarray(x, np.float32).astype(ml_dtypes.bfloat16).astype(np.float64), axis, -1)
    blocks = v.reshape(v.shape[:-1] + (-1, 32))
    amax = np.abs(blocks).max(-1, keepdims=True)
    byte = np.maximum(np.where(amax > 0, np.frexp(amax)[1] - 1 + 127, 0) - down, 1)
    scale = np.exp2(byte - 127.0)
    codes = (blocks / scale).astype(np.float32).astype(dtype).astype(np.float64)
    return np.moveaxis((codes * scale).reshape(v.shape), -1, axis)


WIDE = False


def mx_kscale(k):
    if not WIDE:
        return np.ones(k)
    levels = np.array([10, -10, 5, -5, 0])
    if k % 512:
        return np.exp2(np.random.permutation(np.resize(levels, k // 32))).repeat(32)
    a = np.empty((k // 512, 16))
    for p in range(k // 512):
        a[p, :8] = np.random.permutation(np.resize(levels, 8))
        for g in range(8):
            far = levels[np.abs(levels - a[p, g]) >= 10]
            a[p, g + 8] = far[np.random.randint(len(far))]
    return np.exp2(a.ravel()).repeat(32)


def f64(x):
    return np.asarray(x).astype(np.float64)


def striped(idx):
    return np.tile(np.asarray(idx).reshape(-1, 16).T, (8, 1)).astype(np.uint16)


def unstriped(offs):
    return offs[:16].T.reshape(-1).astype(np.int64)


E2M1 = np.array([0.0, 0.5, 1.0, 1.5, 2.0, 3.0, 4.0, 6.0, -0.0, -0.5, -1.0, -1.5, -2.0, -3.0, -4.0, -6.0])


def pack_weight(w, fmt):
    k, n = w.shape
    w = f64(np.asarray(w, np.float32).astype(ml_dtypes.bfloat16)).reshape(k // 32, 32, n)
    amax = np.abs(w).max(1)
    if fmt == "e4m3":
        byte = np.frexp(amax)[1] - 1 + 127 - 7
    else:
        mant, ex = np.frexp(amax / 6.0)
        byte = np.where(mant > 0.5, ex, ex - 1) + 127
    byte = np.clip(np.where(amax > 0, byte, 1), 1, 254)
    scaled = (w * np.exp2(127.0 - byte)[:, None, :]).reshape(k, n).astype(np.float32)
    by_word = np.ascontiguousarray(scaled.reshape(k // 512, 128, 4, n).transpose(0, 1, 3, 2))
    if fmt == "e4m3":
        words = by_word.astype(ml_dtypes.float8_e4m3fn).view(np.uint8)
    else:
        c = by_word.astype(ml_dtypes.float4_e2m1fn).view(np.uint8) & 0xF
        words = (c[..., 0::2] | (c[..., 1::2] << 4)).reshape(k // 512, 128, 2 * n)
    return np.ascontiguousarray(words), np.ascontiguousarray(byte.astype(np.uint8).reshape(k // 512, 16, n))


def unpack_weight(words, scales, fmt):
    g, _, n = scales.shape
    words = np.ascontiguousarray(words).reshape(g, 128, n, -1)
    if fmt == "e4m3":
        vals = words.view(ml_dtypes.float8_e4m3fn).astype(np.float64)
    else:
        nib = np.empty((g, 128, n, 4), np.uint8)
        nib[..., 0::2] = words & 0xF
        nib[..., 1::2] = words >> 4
        vals = E2M1[nib]
    vals = vals * np.repeat(np.exp2(scales.astype(np.float64) - 127.0), 8, axis=1)[..., None]
    return vals.transpose(0, 1, 3, 2).reshape(g * 512, n)


D, E, T, I, Q = 512, 512, 2048, 512, 128


def setup_inputs():
    n = np.random.standard_normal
    idx = np.random.permutation(T)[:I]
    fd = mx_kscale(D)
    fe = mx_kscale(E)
    keysp = pack_weight(n((D, T)) / fd[:, None], "e4m3")
    valsp = pack_weight(n((E, T)) / fe[:, None], "e4m3")
    return {
        "query": (n((D, Q)) * 0.6 / np.sqrt(D) * fd[:, None]).astype(np.float32),
        "keys_words": keysp[0],
        "keys_scales": keysp[1],
        "lprior": np.tile(np.random.uniform(-7.5, -5.0, T), (128, 1)).astype(np.float32),
        "strict": (np.random.uniform(0.2, 0.8, (Q, 1))).astype(np.float32),
        "gout": (n((E, Q)) * 1 / np.sqrt(E) * fe[:, None]).astype(np.float32),
        "vals_words": valsp[0],
        "vals_scales": valsp[1],
        "dquery": (n((D, Q)) * 1.0 / np.sqrt(D) * fd[:, None]).astype(np.float32),
        "base": (0.5 * n((Q, T))).astype(np.float32),
        "offs": striped(idx),
    }


def reference(query, keys_words, keys_scales, lprior, strict, gout, vals_words, vals_scales, dquery, base, offs):
    idx = unstriped(offs)
    keysu = unpack_weight(keys_words, keys_scales, "e4m3")
    valsu = unpack_weight(vals_words, vals_scales, "e4m3")
    queryq = mxq(f64(query), 0, "e4m3")
    keysidxg = keysu[:, idx]
    a = queryq.T @ keysidxg
    dqueryq = mxq(f64(dquery), 0, "e4m3")
    ta = dqueryq.T @ keysidxg
    b = a - np.max(a, axis=1, keepdims=True)
    p = np.exp(b)
    z = np.sum(p, axis=1, keepdims=True)
    goutq = mxq(f64(gout), 0, "e4m3")
    valsidxg = valsu[:, idx]
    c0 = goutq.T @ valsidxg
    dz = f64(strict) / z - np.sum(p * c0, axis=1, keepdims=True) / np.square(z) - f64(strict) * (-1.0) * np.sum(p * (b - f64(lprior)[:1][:, idx]), axis=1, keepdims=True) / np.square(z)
    dp = 1.0 / z * c0 + f64(strict) * (-1.0) / z * (b - f64(lprior)[:1][:, idx]) + dz
    tb = ta
    tp = tb * p
    tz = np.sum(tp, axis=1, keepdims=True)
    tdz = tz * f64(strict) / np.square(z) * (-1.0) - (np.sum(tp * c0, axis=1, keepdims=True) - tz * z * 2.0 * np.sum(p * c0, axis=1, keepdims=True) / np.square(z)) / np.square(z) - (np.sum(tp * (b - f64(lprior)[:1][:, idx]) + tb * p, axis=1, keepdims=True) * f64(strict) * (-1.0) - tz * z * 2.0 * f64(strict) * (-1.0) * np.sum(p * (b - f64(lprior)[:1][:, idx]), axis=1, keepdims=True) / np.square(z)) / np.square(z)
    tdp = tz * 1.0 / np.square(z) * (-1.0) * c0 + tz * f64(strict) * (-1.0) / np.square(z) * (-1.0) * (b - f64(lprior)[:1][:, idx]) + tb * f64(strict) * (-1.0) / z + tdz
    tdb = tz * f64(strict) * (-1.0) / np.square(z) * (-1.0) * p + tp * f64(strict) * (-1.0) / z + tdp * p + tp * dp
    gs = tdb * 512.0
    gf = np.zeros((Q, T))
    gf[:, idx] = gs
    y = f64(base) + gf
    return y

@@ -1,0 +1,175 @@
+from contextlib import ExitStack
+
+import concourse.mybir as mybir
+from concourse.masks import make_identity
+
+D, T, I, Q = 512, 2048, 512, 128
+FLOPS = 3 * 2 * D * Q * I
+
+F32 = mybir.dt.float32
+BF16 = mybir.dt.bfloat16
+I32 = mybir.dt.int32
+U32 = mybir.dt.uint32
+U16 = mybir.dt.uint16
+U8 = mybir.dt.uint8
+FP8X4 = mybir.dt.float8_e4m3fn_x4
+ALU = mybir.AluOpType
+ACT = mybir.ActivationFunctionType
+
+P = 128
+PACK = 4
+BANK = 512
+GAIN = 512.0
+VALS_ROW = 4
+
+
+def tile_attend_hvpriorpull_s_kernel(
+    tc, query, keys_words, keys_scales, lprior, strict, gout, vals_words, vals_scales, dquery, base, offs, out
+):
+    nc = tc.nc
+    with ExitStack() as ctx:
+        keep = ctx.enter_context(tc.tile_pool(name="keep", bufs=1))
+        psum = ctx.enter_context(tc.psum_pool(name="psum", bufs=1))
+
+        def sb(name, shape, dtype):
+            return keep.tile(shape, dtype, name=name, align_bytes=64)
+
+        offsets = keep.tile([P, I // 16], U16, name="offsets")
+        nc.sync.dma_start(offsets[:], offs)
+
+        def load_scales(name, scales, first_row, queue):
+            plane = keep.tile([P, T], U8, name=name, tag=name, align_bytes=64)
+            nc.vector.memset(plane[:].bitcast(I32), 0)
+            for quad in range(4):
+                row = 32 * quad + first_row
+                queue.dma_start(
+                    plane[row : row + 4, :].bitcast(I32), scales[0, 4 * quad : 4 * quad + 4, :].bitcast(I32)
+                )
+            return plane
+
+        def load_words(name, words, tag):
+            pool_words = keep.tile([P, T], U32, name=name, tag=tag, align_bytes=64)
+            nc.sync.dma_start(pool_words[:].bitcast(I32), words[0].rearrange("p n t -> p (n t)").bitcast(I32))
+            return pool_words
+
+        def load_rows(name, rows, tag):
+            raw = keep.tile([P, PACK, Q], F32, name=name, tag=tag, align_bytes=64)
+            nc.sync.dma_start(raw[:], rows.rearrange("(p j) w -> p j w", j=PACK))
+            return raw
+
+        def interleave(name, raw):
+            grouped = sb(name, [P, Q, PACK], BF16)
+            nc.scalar.copy(
+                grouped[:].rearrange("p (c i) j -> p c j i", i=4), raw[:].rearrange("p j (c i) -> p c j i", i=4)
+            )
+            return grouped
+
+        def quantize(name, grouped):
+            codes = sb(name + "_codes", [P, Q], U32)
+            scales = sb(name + "_scales", [P, Q], U8)
+            nc.vector.quantize_mx(
+                out=codes[:].bitcast(FP8X4), scales=scales[:], in_=grouped[:].rearrange("p w j -> p (w j)")
+            )
+            return codes, scales
+
+        def gather(name, window, dtype, tag):
+            listed = keep.tile([P, I], dtype, name=name, tag=tag, align_bytes=64)
+            nc.vector.tensor_copy(listed[:], window[:].indirect(offsets[:]))
+            return listed
+
+        def product(name, rows, words, scales):
+            acc = psum.tile([Q, I], F32, name=name)
+            nc.tensor.matmul_mx(
+                out=acc[:],
+                lhsT=rows[0][:].bitcast(FP8X4),
+                lhsT_scale=rows[1][:],
+                rhs=words[:].bitcast(FP8X4),
+                rhs_scale=scales,
+                start=True,
+                stop=True,
+            )
+            return acc
+
+        def column(name):
+            return keep.tile([P, 1], F32, name=name)
+
+        key_plane = load_scales("key_plane", keys_scales, 0, nc.sync)
+        lp16 = sb("lp16", [P, T // P], F32)
+        nc.sync.dma_start(lp16[:], lprior[0].rearrange("(p c) -> p c", p=P))
+        q_raw = load_rows("q_raw", query, "q_raw")
+        key_pool = load_words("key_pool", keys_words, "key_pool")
+        val_plane = load_scales("val_plane", vals_scales, VALS_ROW, nc.sync)
+        dq_raw = load_rows("dq_raw", dquery, "dq_raw")
+        g_raw = load_rows("g_raw", gout, "g_raw")
+        val_pool = load_words("val_pool", vals_words, "val_pool")
+        s = column("s")
+        nc.sync.dma_start(s[:], strict)
+        base_sb = sb("base_sb", [P, T], F32)
+        nc.sync.dma_start(base_sb[:], base)
+
+        ident = sb("ident", [P, P], F32)
+        make_identity(nc, ident[:])
+        gf = sb("gf", [P, T], F32)
+        nc.vector.memset(gf[:], 0.0)
+        q_grouped = interleave("q_grouped", q_raw)
+        lp_pool = keep.tile([P, T], F32, name="lp_pool", tag="lp_pool", align_bytes=64)
+        lp_view = lp_pool[:].rearrange("q (p b j) -> q b p j", b=4, j=4)
+        for b in range(4):
+            bank = psum.tile([P, 4, P], F32, name="lp_bank%d" % b)
+            for j in range(4):
+                c = 4 * b + j
+                nc.tensor.transpose(bank[:, j, :], lp16[:, c : c + 1].to_broadcast([P, P]), ident[:])
+            nc.scalar.copy(lp_view[:, b], bank[:].rearrange("q j p -> q p j"))
+
+        key_scales = gather("key_scales", key_plane, U8, "key_scales")
+        q_mx = quantize("q", q_grouped)
+        key_words = gather("key_words", key_pool, U32, "key_words")
+        a = product("a", q_mx, key_words, key_scales[:])
+        val_scales = gather("val_scales", val_plane, U8, "key_pool")
+        dq_mx = quantize("dq", interleave("dq_grouped", dq_raw))
+        g_mx = quantize("g", interleave("g_grouped", g_raw))
+        ta = product("ta", dq_mx, key_words, key_scales[:])
+
+        neg_a = sb("neg_a", [P, I], F32)
+        neg_max = column("neg_max")
+        nc.vector.tensor_scalar(neg_a[:], a[:], -1.0, None, ALU.mult, ALU.min, accum_out=neg_max[:])
+        p = sb("p", [P, I], F32)
+        z = column("z")
+        nc.scalar.activation(p[:], neg_a[:], ACT.Exp, bias=neg_max[:], scale=-1.0, accum_out=z[:])
+        d = sb("d", [P, I], F32)
+        nc.vector.tensor_tensor(d[:], lp_pool[:].indirect(offsets[:]), neg_a[:], ALU.add)
+
+        inv_z = column("inv_z")
+        nc.vector.reciprocal(inv_z[:], z[:])
+        share = sb("share", [P, I], F32)
+        nc.scalar.activation(share[:], p[:], ACT.Copy, scale=inv_z[:])
+        share_gain = sb("share_gain", [P, I], F32)
+        nc.scalar.activation(share_gain[:], share[:], ACT.Copy, scale=GAIN)
+        neg_share = sb("neg_share", [P, I], F32)
+        nc.scalar.activation(neg_share[:], share[:], ACT.Copy, scale=-1.0)
+
+        val_words = gather("val_words", val_pool, U32, "val_words")
+        c0 = product("c0", g_mx, val_words, val_scales[VALS_ROW:, :])
+
+        t_terms = keep.tile([P, I], F32, name="t_terms", tag="val_pool", align_bytes=64)
+        t_mean = column("t_mean")
+        nc.vector.scalar_tensor_tensor(t_terms[:], ta[:], 1.0, share[:], ALU.mult, ALU.mult, accum_out=t_mean[:])
+        u = sb("u", [P, I], F32)
+        nc.vector.scalar_tensor_tensor(u[:], d[:], s[:], c0[:], ALU.mult, ALU.add)
+        e = sb("e", [P, I], F32)
+        nc.vector.scalar_tensor_tensor(e[:], ta[:], t_mean[:], share_gain[:], ALU.subtract, ALU.mult)
+        u_terms = sb("u_terms", [P, I], F32)
+        u_shift = column("u_shift")
+        nc.vector.scalar_tensor_tensor(u_terms[:], u[:], s[:], share[:], ALU.add, ALU.mult, accum_out=u_shift[:])
+        x = sb("x", [P, I], F32)
+        cov = column("cov")
+        nc.vector.scalar_tensor_tensor(x[:], u[:], u_shift[:], e[:], ALU.subtract, ALU.mult, accum_out=cov[:])
+        n = sb("n", [P, I], F32)
+        nc.scalar.activation(n[:], neg_share[:], ACT.Copy, scale=cov[:])
+        nc.vector.tensor_tensor(gf[:].indirect(offsets[:]), x[:], n[:], ALU.add)
+
+        for k in range(T // BANK):
+            cols = slice(k * BANK, (k + 1) * BANK)
+            y = sb("y%d" % k, [P, BANK], F32)
+            nc.vector.tensor_tensor(y[:], gf[:, cols], base_sb[:, cols], ALU.add)
+            nc.sync.dma_start(out[:, cols], y[:])

@@ -47,9 +47,11 @@ def tile_attend_hvpriorpull_s_kernel(
                 )
             return plane
 
-        def load_words(name, words, tag):
+        def load_words(name, words, tag, cuts):
             pool_words = keep.tile([P, T], U32, name=name, tag=tag, align_bytes=64)
-            nc.sync.dma_start(pool_words[:].bitcast(I32), words[0].rearrange("p n t -> p (n t)").bitcast(I32))
+            source = words[0].rearrange("p n t -> p (n t)").bitcast(I32)
+            for lo, hi in zip(cuts, cuts[1:]):
+                nc.sync.dma_start(pool_words[:, lo:hi].bitcast(I32), source[:, lo:hi])
             return pool_words
 
         def load_rows(name, rows, tag):
@@ -97,11 +99,11 @@ def tile_attend_hvpriorpull_s_kernel(
         lp16 = sb("lp16", [P, T // P], F32)
         nc.sync.dma_start(lp16[:], lprior[0].rearrange("(p c) -> p c", p=P))
         q_raw = load_rows("q_raw", query, "q_raw")
-        key_pool = load_words("key_pool", keys_words, "key_pool")
+        key_pool = load_words("key_pool", keys_words, "key_pool", (0, 1280, T))
         val_plane = load_scales("val_plane", vals_scales, VALS_ROW, nc.sync)
         dq_raw = load_rows("dq_raw", dquery, "dq_raw")
         g_raw = load_rows("g_raw", gout, "g_raw")
-        val_pool = load_words("val_pool", vals_words, "val_pool")
+        val_pool = load_words("val_pool", vals_words, "val_pool", (0, T))
         s = column("s")
         nc.sync.dma_start(s[:], strict)
         base_sb = sb("base_sb", [P, T], F32)
@@ -112,7 +114,7 @@ def tile_attend_hvpriorpull_s_kernel(
         gf = sb("gf", [P, T], F32)
         nc.vector.memset(gf[:], 0.0)
         q_grouped = interleave("q_grouped", q_raw)
-        lp_pool = keep.tile([P, T], F32, name="lp_pool", tag="lp_pool", align_bytes=64)
+        lp_pool = keep.tile([P, T], F32, name="lp_pool", tag="q_raw", align_bytes=64)
         lp_view = lp_pool[:].rearrange("q (p b j) -> q b p j", b=4, j=4)
         for b in range(4):
             bank = psum.tile([P, 4, P], F32, name="lp_bank%d" % b)
@@ -145,8 +147,6 @@ def tile_attend_hvpriorpull_s_kernel(
         nc.scalar.activation(share[:], p[:], ACT.Copy, scale=inv_z[:])
         share_gain = sb("share_gain", [P, I], F32)
         nc.scalar.activation(share_gain[:], share[:], ACT.Copy, scale=GAIN)
-        neg_share = sb("neg_share", [P, I], F32)
-        nc.scalar.activation(neg_share[:], share[:], ACT.Copy, scale=-1.0)
 
         val_words = gather("val_words", val_pool, U32, "val_words")
         c0 = product("c0", g_mx, val_words, val_scales[VALS_ROW:, :])
@@ -165,11 +165,12 @@ def tile_attend_hvpriorpull_s_kernel(
         cov = column("cov")
         nc.vector.scalar_tensor_tensor(x[:], u[:], u_shift[:], e[:], ALU.subtract, ALU.mult, accum_out=cov[:])
         n = sb("n", [P, I], F32)
-        nc.scalar.activation(n[:], neg_share[:], ACT.Copy, scale=cov[:])
+        nc.vector.tensor_scalar(n[:], share[:], cov[:], -1.0, ALU.mult, ALU.mult)
         nc.vector.tensor_tensor(gf[:].indirect(offsets[:]), x[:], n[:], ALU.add)
 
-        for k in range(T // BANK):
-            cols = slice(k * BANK, (k + 1) * BANK)
-            y = sb("y%d" % k, [P, BANK], F32)
+        cuts = (0, 256, 768, 1280, 1792, T)
+        for lo, hi in zip(cuts, cuts[1:]):
+            cols = slice(lo, hi)
+            y = sb("y%d" % lo, [P, hi - lo], F32)
             nc.vector.tensor_tensor(y[:], gf[:, cols], base_sb[:, cols], ALU.add)
             nc.sync.dma_start(out[:, cols], y[:])

from contextlib import ExitStack

import concourse.mybir as mybir
from concourse.masks import make_identity

D, T, I, Q = 512, 2048, 512, 128
FLOPS = 3 * 2 * D * Q * I

F32 = mybir.dt.float32
BF16 = mybir.dt.bfloat16
I32 = mybir.dt.int32
U32 = mybir.dt.uint32
U16 = mybir.dt.uint16
U8 = mybir.dt.uint8
FP8X4 = mybir.dt.float8_e4m3fn_x4
ALU = mybir.AluOpType
ACT = mybir.ActivationFunctionType

P = 128
PACK = 4
BANK = 512
GAIN = 512.0
VALS_ROW = 4


def tile_attend_hvpriorpull_s_kernel(
    tc, query, keys_words, keys_scales, lprior, strict, gout, vals_words, vals_scales, dquery, base, offs, out
):
    nc = tc.nc
    with ExitStack() as ctx:
        keep = ctx.enter_context(tc.tile_pool(name="keep", bufs=1))
        psum = ctx.enter_context(tc.psum_pool(name="psum", bufs=1))

        def sb(name, shape, dtype):
            return keep.tile(shape, dtype, name=name, align_bytes=64)

        offsets = keep.tile([P, I // 16], U16, name="offsets")
        nc.sync.dma_start(offsets[:], offs)

        def load_scales(name, scales, first_row, queue):
            plane = keep.tile([P, T], U8, name=name, tag=name, align_bytes=64)
            nc.vector.memset(plane[:].bitcast(I32), 0)
            for quad in range(4):
                row = 32 * quad + first_row
                queue.dma_start(
                    plane[row : row + 4, :].bitcast(I32), scales[0, 4 * quad : 4 * quad + 4, :].bitcast(I32)
                )
            return plane

        def load_words(name, words, tag, cuts):
            pool_words = keep.tile([P, T], U32, name=name, tag=tag, align_bytes=64)
            source = words[0].rearrange("p n t -> p (n t)").bitcast(I32)
            for lo, hi in zip(cuts, cuts[1:]):
                nc.sync.dma_start(pool_words[:, lo:hi].bitcast(I32), source[:, lo:hi])
            return pool_words

        def load_rows(name, rows, tag):
            raw = keep.tile([P, PACK, Q], F32, name=name, tag=tag, align_bytes=64)
            nc.sync.dma_start(raw[:], rows.rearrange("(p j) w -> p j w", j=PACK))
            return raw

        def interleave(name, raw):
            grouped = sb(name, [P, Q, PACK], BF16)
            nc.scalar.copy(
                grouped[:].rearrange("p (c i) j -> p c j i", i=4), raw[:].rearrange("p j (c i) -> p c j i", i=4)
            )
            return grouped

        def quantize(name, grouped):
            codes = sb(name + "_codes", [P, Q], U32)
            scales = sb(name + "_scales", [P, Q], U8)
            nc.vector.quantize_mx(
                out=codes[:].bitcast(FP8X4), scales=scales[:], in_=grouped[:].rearrange("p w j -> p (w j)")
            )
            return codes, scales

        def gather(name, window, dtype, tag):
            listed = keep.tile([P, I], dtype, name=name, tag=tag, align_bytes=64)
            nc.vector.tensor_copy(listed[:], window[:].indirect(offsets[:]))
            return listed

        def product(name, rows, words, scales):
            acc = psum.tile([Q, I], F32, name=name)
            nc.tensor.matmul_mx(
                out=acc[:],
                lhsT=rows[0][:].bitcast(FP8X4),
                lhsT_scale=rows[1][:],
                rhs=words[:].bitcast(FP8X4),
                rhs_scale=scales,
                start=True,
                stop=True,
            )
            return acc

        def column(name):
            return keep.tile([P, 1], F32, name=name)

        key_plane = load_scales("key_plane", keys_scales, 0, nc.sync)
        lp16 = sb("lp16", [P, T // P], F32)
        nc.sync.dma_start(lp16[:], lprior[0].rearrange("(p c) -> p c", p=P))
        q_raw = load_rows("q_raw", query, "q_raw")
        key_pool = load_words("key_pool", keys_words, "key_pool", (0, 1280, T))
        val_plane = load_scales("val_plane", vals_scales, VALS_ROW, nc.sync)
        dq_raw = load_rows("dq_raw", dquery, "dq_raw")
        g_raw = load_rows("g_raw", gout, "g_raw")
        val_pool = load_words("val_pool", vals_words, "val_pool", (0, T))
        s = column("s")
        nc.sync.dma_start(s[:], strict)
        base_sb = sb("base_sb", [P, T], F32)
        nc.sync.dma_start(base_sb[:], base)

        ident = sb("ident", [P, P], F32)
        make_identity(nc, ident[:])
        gf = sb("gf", [P, T], F32)
        nc.vector.memset(gf[:], 0.0)
        q_grouped = interleave("q_grouped", q_raw)
        lp_pool = keep.tile([P, T], F32, name="lp_pool", tag="q_raw", align_bytes=64)
        lp_view = lp_pool[:].rearrange("q (p b j) -> q b p j", b=4, j=4)
        for b in range(4):
            bank = psum.tile([P, 4, P], F32, name="lp_bank%d" % b)
            for j in range(4):
                c = 4 * b + j
                nc.tensor.transpose(bank[:, j, :], lp16[:, c : c + 1].to_broadcast([P, P]), ident[:])
            nc.scalar.copy(lp_view[:, b], bank[:].rearrange("q j p -> q p j"))

        key_scales = gather("key_scales", key_plane, U8, "key_scales")
        q_mx = quantize("q", q_grouped)
        key_words = gather("key_words", key_pool, U32, "key_words")
        a = product("a", q_mx, key_words, key_scales[:])
        val_scales = gather("val_scales", val_plane, U8, "key_pool")
        dq_mx = quantize("dq", interleave("dq_grouped", dq_raw))
        g_mx = quantize("g", interleave("g_grouped", g_raw))
        ta = product("ta", dq_mx, key_words, key_scales[:])

        neg_a = sb("neg_a", [P, I], F32)
        neg_max = column("neg_max")
        nc.vector.tensor_scalar(neg_a[:], a[:], -1.0, None, ALU.mult, ALU.min, accum_out=neg_max[:])
        p = sb("p", [P, I], F32)
        z = column("z")
        nc.scalar.activation(p[:], neg_a[:], ACT.Exp, bias=neg_max[:], scale=-1.0, accum_out=z[:])
        d = sb("d", [P, I], F32)
        nc.vector.tensor_tensor(d[:], lp_pool[:].indirect(offsets[:]), neg_a[:], ALU.add)

        inv_z = column("inv_z")
        nc.vector.reciprocal(inv_z[:], z[:])
        share = sb("share", [P, I], F32)
        nc.scalar.activation(share[:], p[:], ACT.Copy, scale=inv_z[:])
        share_gain = sb("share_gain", [P, I], F32)
        nc.scalar.activation(share_gain[:], share[:], ACT.Copy, scale=GAIN)

        val_words = gather("val_words", val_pool, U32, "val_words")
        c0 = product("c0", g_mx, val_words, val_scales[VALS_ROW:, :])

        t_terms = keep.tile([P, I], F32, name="t_terms", tag="val_pool", align_bytes=64)
        t_mean = column("t_mean")
        nc.vector.scalar_tensor_tensor(t_terms[:], ta[:], 1.0, share[:], ALU.mult, ALU.mult, accum_out=t_mean[:])
        u = sb("u", [P, I], F32)
        nc.vector.scalar_tensor_tensor(u[:], d[:], s[:], c0[:], ALU.mult, ALU.add)
        e = sb("e", [P, I], F32)
        nc.vector.scalar_tensor_tensor(e[:], ta[:], t_mean[:], share_gain[:], ALU.subtract, ALU.mult)
        u_terms = sb("u_terms", [P, I], F32)
        u_shift = column("u_shift")
        nc.vector.scalar_tensor_tensor(u_terms[:], u[:], s[:], share[:], ALU.add, ALU.mult, accum_out=u_shift[:])
        x = sb("x", [P, I], F32)
        cov = column("cov")
        nc.vector.scalar_tensor_tensor(x[:], u[:], u_shift[:], e[:], ALU.subtract, ALU.mult, accum_out=cov[:])
        n = sb("n", [P, I], F32)
        nc.vector.tensor_scalar(n[:], share[:], cov[:], -1.0, ALU.mult, ALU.mult)
        nc.vector.tensor_tensor(gf[:].indirect(offsets[:]), x[:], n[:], ALU.add)

        cuts = (0, 256, 768, 1280, 1792, T)
        for lo, hi in zip(cuts, cuts[1:]):
            cols = slice(lo, hi)
            y = sb("y%d" % lo, [P, hi - lo], F32)
            nc.vector.tensor_tensor(y[:], gf[:, cols], base_sb[:, cols], ALU.add)
            nc.sync.dma_start(out[:, cols], y[:])
